import numpy as np
import ml_dtypes


def mxq(x, axis, fmt="e4m3"):
    dtype, down = {"e4m3": (ml_dtypes.float8_e4m3fn, 7), "e5m2": (ml_dtypes.float8_e5m2, 14)}[fmt]
    v = np.moveaxis(np.asarray(x, np.float32).astype(ml_dtypes.bfloat16).astype(np.float64), axis, -1)
    blocks = v.reshape(v.shape[:-1] + (-1, 32))
    amax = np.abs(blocks).max(-1, keepdims=True)
    byte = np.maximum(np.where(amax > 0, np.frexp(amax)[1] - 1 + 127, 0) - down, 1)
    scale = np.exp2(byte - 127.0)
    codes = (blocks / scale).astype(np.float32).astype(dtype).astype(np.float64)
    return np.moveaxis((codes * scale).reshape(v.shape), -1, axis)


WIDE = False


def mx_kscale(k):
    if not WIDE:
        return np.ones(k)
    levels = np.array([10, -10, 5, -5, 0])
    if k % 512:
        return np.exp2(np.random.permutation(np.resize(levels, k // 32))).repeat(32)
    a = np.empty((k // 512, 16))
    for p in range(k // 512):
        a[p, :8] = np.random.permutation(np.resize(levels, 8))
        for g in range(8):
            far = levels[np.abs(levels - a[p, g]) >= 10]
            a[p, g + 8] = far[np.random.randint(len(far))]
    return np.exp2(a.ravel()).repeat(32)


def f64(x):
    return np.asarray(x).astype(np.float64)


def striped(idx):
    return np.tile(idx.reshape(-1, 16).T, (8, 1)).astype(np.uint16)


def unstriped(offs):
    return offs[:16].T.reshape(-1).astype(np.int64)


E2M1 = np.array([0.0, 0.5, 1.0, 1.5, 2.0, 3.0, 4.0, 6.0, -0.0, -0.5, -1.0, -1.5, -2.0, -3.0, -4.0, -6.0])


def pack_weight(w, fmt):
    k, n = w.shape
    w = f64(np.asarray(w, np.float32).astype(ml_dtypes.bfloat16)).reshape(k // 32, 32, n)
    amax = np.abs(w).max(1)
    if fmt == "e4m3":
        byte = np.frexp(amax)[1] - 1 + 127 - 7
    else:
        mant, ex = np.frexp(amax / 6.0)
        byte = np.where(mant > 0.5, ex, ex - 1) + 127
    byte = np.clip(np.where(amax > 0, byte, 1), 1, 254)
    scaled = (w * np.exp2(127.0 - byte)[:, None, :]).reshape(k, n).astype(np.float32)
    by_word = np.ascontiguousarray(scaled.reshape(k // 512, 128, 4, n).transpose(0, 1, 3, 2))
    if fmt == "e4m3":
        words = by_word.astype(ml_dtypes.float8_e4m3fn).view(np.uint8)
    else:
        c = by_word.astype(ml_dtypes.float4_e2m1fn).view(np.uint8) & 0xF
        words = (c[..., 0::2] | (c[..., 1::2] << 4)).reshape(k // 512, 128, 2 * n)
    return np.ascontiguousarray(words), np.ascontiguousarray(byte.astype(np.uint8).reshape(k // 512, 16, n))


def unpack_weight(words, scales, fmt):
    g, _, n = scales.shape
    words = np.ascontiguousarray(words).reshape(g, 128, n, -1)
    if fmt == "e4m3":
        vals = words.view(ml_dtypes.float8_e4m3fn).astype(np.float64)
    else:
        nib = np.empty((g, 128, n, 4), np.uint8)
        nib[..., 0::2] = words & 0xF
        nib[..., 1::2] = words >> 4
        vals = E2M1[nib]
    vals = vals * np.repeat(np.exp2(scales.astype(np.float64) - 127.0), 8, axis=1)[..., None]
    return vals.transpose(0, 1, 3, 2).reshape(g * 512, n)


def gelu(v):
    return 0.5 * v * (1.0 + np.tanh(np.sqrt(2.0 / np.pi) * (v + 0.044715 * v**3)))


K, H, N, T, S, T2, P = 1024, 512, 384, 2048, 1024, 2048, 1024


def setup_inputs():
    n = np.random.standard_normal
    s = mx_kscale(K)[:, None]
    u = mx_kscale(H)[:, None]
    tab_words, tab_scales = pack_weight(n((K, T)) * s, "e4m3")
    w1 = (0.65 * n((K, H)) / np.sqrt(K) / s).astype(np.float32)
    w2_words, w2_scales = pack_weight(0.55 * n((K, H)) / np.sqrt(K) / s, "e2m1")
    w3_words, w3_scales = pack_weight(n((H, N)) / np.sqrt(H) / u, "e4m3")
    w4 = (n((H, N)) / np.sqrt(H) / u).astype(np.float32)
    sign = np.random.choice([-1.0, 1.0], H)
    return {
        "tab_words": tab_words, "tab_scales": tab_scales,
        "offs": striped(np.random.permutation(T)[:S]),
        "offs2": striped(np.random.permutation(T2)[:S]),
        "offs3": striped(np.random.permutation(T2)[:P]),
        "w1": w1, "w2_words": w2_words, "w2_scales": w2_scales,
        "page0": (0.8 * n((H, T2))).astype(np.float32),
        "wgs": np.exp(0.3 * n((128, S))).astype(np.float32),
        "slope": np.random.uniform(1, 3, H).astype(np.float32),
        "share": np.random.uniform(0.1, 0.5, H).astype(np.float32),
        "wear": (0.25 * n((H, P))).astype(np.float32),
        "gain": (sign * np.random.uniform(1.5, 3.5, H) * u[:, 0]).astype(np.float32),
        "w3_words": w3_words, "w3_scales": w3_scales, "w4": w4,
        "bias": (0.5 * n(N)).astype(np.float32),
    }


def reference(tab_words, tab_scales, offs, offs2, offs3, w1, w2_words, w2_scales, page0, wgs,
              slope, share, wear, gain, w3_words, w3_scales, w4, bias):
    v = unpack_weight(tab_words, tab_scales, "e4m3")[:, unstriped(offs)]
    x1 = mxq(f64(w1), 0, "e4m3").T @ v
    x2 = unpack_weight(w2_words, w2_scales, "e2m1").T @ v
    h = x1 - np.abs(x2)
    page = f64(page0).copy()
    page[:, unstriped(offs2)] = np.tile(f64(wgs), (H // 128, 1)) * h
    top = page.max(axis=1)
    a = 1.0 / (1.0 + np.exp(-f64(slope)[:, None] * (page[:, unstriped(offs3)] - f64(share)[:, None] * top[:, None])))
    q = mxq(f64(gain)[:, None] * (a - f64(wear)), 0, "e4m3")
    y3 = unpack_weight(w3_words, w3_scales, "e4m3").T @ q
    y4 = mxq(f64(w4), 0, "e4m3").T @ q
    return y3 * y4 + f64(bias)[:, None]

@@ -1,0 +1,320 @@
+from contextlib import ExitStack
+
+import concourse.mybir as mybir
+from concourse.masks import make_identity
+
+K, H, N, T, S, T2, M = 1024, 512, 384, 2048, 1024, 2048, 1024
+FLOPS = 2 * (2 * K * H * S + 2 * H * N * M)
+
+F32 = mybir.dt.float32
+BF16 = mybir.dt.bfloat16
+I32 = mybir.dt.int32
+U32 = mybir.dt.uint32
+U16 = mybir.dt.uint16
+U8 = mybir.dt.uint8
+FP8X4 = mybir.dt.float8_e4m3fn_x4
+FP4X4 = mybir.dt.float4_e2m1fn_x4
+ACT = mybir.ActivationFunctionType
+ALU = mybir.AluOpType
+AX = mybir.AxisListType
+
+P = 128
+PACK = 4
+PASSES = K // (P * PACK)
+BANK = 512
+QUADS = 4
+HALVES = S // BANK
+
+
+def tile_list_shedding_alarms_kernel(
+    tc, tab_words, tab_scales, offs, offs2, offs3, w1, w2_words, w2_scales, page0, wgs,
+    slope, share, wear, gain, w3_words, w3_scales, w4, bias, out,
+):
+    nc = tc.nc
+    with ExitStack() as ctx:
+        keep = ctx.enter_context(tc.tile_pool(name="keep", bufs=1))
+        ring = ctx.enter_context(tc.tile_pool(name="ring", bufs=2))
+        psum = ctx.enter_context(tc.psum_pool(name="psum", bufs=1))
+
+        def held(name, shape, dtype):
+            return keep.tile(shape, dtype, name=name, align_bytes=64)
+
+        def bank(number):
+            return psum.tile([P, BANK], F32, name="bank%d" % number)
+
+        def entries(offsets, first, count):
+            return offsets[:, first // 16 : (first + count) // 16]
+
+        tab_s = held("tab_s", [P, PASSES * T], U8)
+        nc.vector.memset(tab_s[:].bitcast(I32), 0)
+        w2s_raw = held("w2s_raw", [P, PASSES * H], U8)
+        nc.vector.memset(w2s_raw[:].bitcast(I32), 0)
+        w3_s = held("w3_s", [P, N], U8)
+        nc.vector.memset(w3_s[:].bitcast(I32), 0)
+
+        list1 = held("list1", [P, S // 16], U16)
+        nc.sync.dma_start(list1[:], offs)
+        tab_w = [held("tab_w%d" % a, [P, T], U32) for a in range(PASSES)]
+
+        def load_table(a):
+            nc.sync.dma_start(tab_w[a][:].bitcast(I32), tab_words[a].rearrange("p t i -> p (t i)").bitcast(I32))
+
+        load_table(0)
+        for q in range(QUADS):
+            nc.gpsimd.dma_start(
+                tab_s[32 * q : 32 * q + 4, :].bitcast(I32).rearrange("r (a c) -> r a c", a=PASSES),
+                tab_scales[:, 4 * q : 4 * q + 4, :].bitcast(I32).rearrange("a r c -> r a c"),
+            )
+        for q in range(QUADS):
+            nc.scalar.dma_start(
+                w2s_raw[32 * q : 32 * q + 4, :].bitcast(I32).rearrange("r (a c) -> r a c", a=PASSES),
+                w2_scales[:, 4 * q : 4 * q + 4, :].bitcast(I32).rearrange("a r c -> r a c"),
+            )
+        ident = held("ident", [P, P], F32)
+        make_identity(nc, ident[:])
+        w1_rows = w1.rearrange("(a p j) c -> a p j c", a=PASSES, j=PACK)
+        w1_raw0 = held("w1_raw0", [P, PACK, H], F32)
+        nc.sync.dma_start(w1_raw0[:], w1_rows[0])
+        w2w_raw = held("w2w_raw", [P, PASSES * H], U16)
+        nc.sync.dma_start(
+            w2w_raw[:].bitcast(I32).rearrange("p (a c) -> p a c", a=PASSES),
+            w2_words.bitcast(I32).rearrange("a p c -> p a c"),
+        )
+        load_table(1)
+        w1_raw1 = [held("w1_raw1_%d" % u, [P, PACK, H // 2], F32) for u in range(2)]
+        for u in range(2):
+            nc.sync.dma_start(w1_raw1[u][:], w1_rows[1][:, :, H // 2 * u : H // 2 * (u + 1)])
+        list2 = held("list2", [P, S // 16], U16)
+        nc.sync.dma_start(list2[:], offs2)
+        wgs_rows = wgs.rearrange("(i t) c -> i t c", t=PACK)
+        wg_first = [held("wg_first%d" % c, [P, BANK], F32) for c in range(HALVES)]
+
+        def load_first_weights(c):
+            for q in (0, 2, 1, 3):
+                nc.sync.dma_start(wg_first[c][32 * q : 32 * q + 32, :], wgs_rows[:, 0, BANK * c : BANK * (c + 1)])
+
+        load_first_weights(0)
+        page_rows = page0.rearrange("(p t) c -> t p c", t=PACK)
+        wear_rows = wear.rearrange("(p t) c -> t p c", t=PACK)
+        pages = [held("page%d" % t, [P, T2], F32) for t in range(PACK)]
+        wears = [held("wear%d" % t, [P, M], F32) for t in range(PACK)]
+        nc.sync.dma_start(pages[0][:], page_rows[0])
+        load_first_weights(1)
+
+        v_w = [[held("v_w%d_%d" % (a, c), [P, BANK], U32) for c in range(HALVES)] for a in range(PASSES)]
+
+        def gather_words(a):
+            for c in range(HALVES):
+                nc.vector.tensor_copy(v_w[a][c][:], tab_w[a][:].indirect(entries(list1, BANK * c, BANK)))
+
+        gather_words(0)
+        v_planes = [held("v_s%d" % a, [P, S], U8) for a in range(PASSES)]
+        for a in range(PASSES):
+            nc.vector.tensor_copy(v_planes[a][:], tab_s[:, T * a : T * (a + 1)].indirect(list1[:]))
+
+        wg_rest = held("wg_rest", [P, PACK - 1, S], F32)
+        for q in (0, 2, 1, 3):
+            nc.sync.dma_start(wg_rest[32 * q : 32 * q + 32, :, :], wgs_rows[:, 1:, :])
+        nc.sync.dma_start(pages[1][:], page_rows[1])
+        list3 = held("list3", [P, M // 16], U16)
+        nc.sync.dma_start(list3[:], offs3)
+        slope_c = held("slope_c", [P, PACK], F32)
+        share_c = held("share_c", [P, PACK], F32)
+        gain_c = held("gain_c", [P, PACK], F32)
+        for col, vec in ((slope_c, slope), (share_c, share), (gain_c, gain)):
+            nc.sync.dma_start(col[:], vec.rearrange("(p t) -> p t", t=PACK))
+        nc.sync.dma_start(wears[0][:], wear_rows[0])
+        nc.sync.dma_start(pages[2][:], page_rows[2])
+        for t in range(1, PACK):
+            nc.sync.dma_start(wears[t][:], wear_rows[t])
+        w4_raw = held("w4_raw", [P, PACK, N], F32)
+        nc.sync.dma_start(w4_raw[:], w4.rearrange("(p j) c -> p j c", j=PACK))
+        w3_w = held("w3_w", [P, N], U32)
+        nc.sync.dma_start(w3_w[:].bitcast(I32), w3_words[0].rearrange("p c i -> p (c i)").bitcast(I32))
+        for q in range(QUADS):
+            nc.sync.dma_start(w3_s[32 * q : 32 * q + 4, :].bitcast(I32), w3_scales[0, 4 * q : 4 * q + 4, :].bitcast(I32))
+        bias_c = held("bias_c", [P, N // P], F32)
+        with nc.allow_non_contiguous_dma(reason="one value a partition"):
+            nc.sync.dma_start(bias_c[:], bias.rearrange("(c p) -> p c", p=P))
+        nc.sync.dma_start(pages[3][:], page_rows[3])
+
+        w2_s = held("w2_s", [P, PASSES * H], U8)
+        nc.gpsimd.tensor_copy(
+            w2_s[:].rearrange("p (a t m) -> p a t m", a=PASSES, t=PACK),
+            w2s_raw[:].rearrange("p (a m t) -> p a t m", a=PASSES, t=PACK),
+        )
+        w1_w = [held("w1_w%d" % a, [P, H], U32) for a in range(PASSES)]
+        w1_s = [held("w1_s%d" % a, [P, H], U8) for a in range(PASSES)]
+        w1_bf = [held("w1_bf%d" % a, [P, H * PACK], BF16) for a in range(PASSES)]
+        dealt = [w1_bf[a][:].rearrange("p (t m j) -> p m j t", t=PACK, j=PACK) for a in range(PASSES)]
+        nc.scalar.copy(dealt[0], w1_raw0[:].rearrange("p j (m t) -> p m j t", t=PACK))
+        w2_w = held("w2_w", [P, PASSES * H], U16)
+        nc.scalar.copy(
+            w2_w[:].rearrange("p (a t m) -> p a m t", a=PASSES, t=PACK),
+            w2w_raw[:].rearrange("p (a m t) -> p a m t", a=PASSES, t=PACK),
+        )
+        nc.vector.quantize_mx(out=w1_w[0][:].bitcast(FP8X4), scales=w1_s[0][:], in_=w1_bf[0][:])
+        gather_words(1)
+        for u in range(2):
+            nc.scalar.copy(dealt[1][:, P // 2 * u : P // 2 * (u + 1)], w1_raw1[u][:].rearrange("p j (m t) -> p m j t", t=PACK))
+        nc.vector.quantize_mx(out=w1_w[1][:, :P].bitcast(FP8X4), scales=w1_s[1][:, :P], in_=w1_bf[1][:, : P * PACK])
+
+        def w1_slice(a, t):
+            rows = slice(P * t, P * (t + 1))
+            return w1_w[a][:, rows].bitcast(FP8X4), w1_s[a][:, rows]
+
+        def w2_slice(a, t):
+            rows = slice(H * a + P * t, H * a + P * (t + 1))
+            return w2_w[:, rows].bitcast(FP4X4), w2_s[:, rows]
+
+        def direct_pass(acc, weight, a, c):
+            codes, scales = weight(a, 0)
+            nc.tensor.matmul_mx(
+                out=acc[:], lhsT=codes, lhsT_scale=scales,
+                rhs=v_w[a][c][:].bitcast(FP8X4), rhs_scale=v_planes[a][:, BANK * c : BANK * (c + 1)],
+                start=(a == 0), stop=(a == PASSES - 1),
+            )
+
+        def scores_turned(t, c, h):
+            x2 = bank(4 + 2 * c)
+            x1 = bank(5 + 2 * c)
+            for acc, weight in ((x2, w2_slice), (x1, w1_slice)):
+                for b in range(BANK // P):
+                    for a in range(PASSES):
+                        codes, scales = weight(a, t)
+                        nc.tensor.matmul_mx(
+                            out=acc[:, P * b : P * (b + 1)],
+                            lhsT=v_w[a][c][:, P * b : P * (b + 1)].bitcast(FP8X4),
+                            lhsT_scale=v_planes[a][:, BANK * c + P * b : BANK * c + P * (b + 1)],
+                            rhs=codes, rhs_scale=scales,
+                            start=(a == 0), stop=(a == PASSES - 1),
+                        )
+            mag = held("mag%d_%d" % (t, c), [P, BANK], F32)
+            nc.scalar.activation(mag[:], x2[:], ACT.Abs)
+            neg = ring.tile([P, BANK], F32, name="neg")
+            nc.scalar.activation(neg[:], x1[:], ACT.Copy, scale=-1.0)
+            total = bank(c)
+            for b in range(BANK // P):
+                block = slice(P * b, P * (b + 1))
+                nc.tensor.matmul(total[:, block], mag[:, block], ident[:], start=True, stop=False, is_transpose=True)
+                nc.tensor.matmul(total[:, block], neg[:, block], ident[:], start=False, stop=True, is_transpose=True)
+            nc.scalar.activation(h[:, BANK * c : BANK * (c + 1)], total[:], ACT.Copy, scale=-1.0)
+
+        first = [(bank(2 * c), bank(2 * c + 1)) for c in range(HALVES)]
+        mags = []
+        for c in range(HALVES):
+            x2, x1 = first[c]
+            direct_pass(x2, w2_slice, 0, c)
+            direct_pass(x1, w1_slice, 0, c)
+            direct_pass(x2, w2_slice, 1, c)
+            mag = ring.tile([P, BANK], F32, name="mag")
+            nc.scalar.activation(mag[:], x2[:], ACT.Abs)
+            mags.append(mag)
+        for c in range(HALVES):
+            direct_pass(first[c][1], w1_slice, 1, c)
+        for c in range(HALVES):
+            h = held("h_first", [P, BANK], F32)
+            nc.vector.tensor_tensor(h[:], first[c][1][:], mags[c][:], ALU.subtract)
+            if c == 0:
+                nc.vector.quantize_mx(out=w1_w[1][:, P:].bitcast(FP8X4), scales=w1_s[1][:, P:], in_=w1_bf[1][:, P * PACK :])
+            nc.vector.tensor_tensor(pages[0][:].indirect(entries(list2, BANK * c, BANK)), h[:], wg_first[c][:], ALU.mult)
+        last = PACK - 1
+        hs = [None] + [held("h%d" % t, [P, S], F32) for t in range(1, PACK)]
+        nshare = held("nshare", [P, PACK], F32)
+        nc.gpsimd.tensor_tensor(nshare[:], slope_c[:], share_c[:], ALU.mult)
+        paired = held("paired", [P, PACK // 2, M * 2], BF16)
+        pairs = [paired[:, u, :].rearrange("p (m e) -> p m e", e=2) for u in range(PACK // 2)]
+        both = paired[:].bitcast(F32)
+        tops = held("tops", [P, PACK], F32)
+
+        def opening(t, name):
+            opens = held(name, [P, 1], F32)
+            nc.vector.reduce_max(tops[:, t : t + 1], pages[t][:], AX.X, negate=True)
+            nc.scalar.activation(opens[:], tops[:, t : t + 1], ACT.Copy, scale=nshare[:, t : t + 1])
+            return opens
+
+        def look(t, opens, gate, first, count):
+            nc.scalar.activation(
+                gate[:, first : first + count],
+                pages[t][:].indirect(entries(list3, first, count)),
+                ACT.Sigmoid, bias=opens[:], scale=slope_c[:, t : t + 1],
+            )
+
+        def put(t):
+            nc.vector.tensor_tensor(pages[t][:].indirect(list2[:]), hs[t][:], wg_rest[:, t - 1, :], ALU.mult)
+
+        def scale_wear(t):
+            nc.scalar.activation(wears[t][:], wears[t][:], ACT.Copy, scale=gain_c[:, t : t + 1])
+
+        def early_gate(t, name):
+            opens = opening(t, name)
+            gate = held("gate%d" % (t % 2), [P, M], F32)
+            look(t, opens, gate, 0, M)
+            nc.scalar.activation(gate[:], gate[:], ACT.Copy, scale=gain_c[:, t : t + 1])
+            scale_wear(t)
+            nc.gpsimd.tensor_tensor(pairs[t // 2][:, :, t % 2], gate[:], wears[t][:], ALU.subtract)
+
+        for t in (1, 2):
+            for c in range(HALVES):
+                scores_turned(t, c, hs[t])
+        early_gate(0, "mag2_1")
+        for c in range(HALVES):
+            scores_turned(last, c, hs[last])
+        put(1)
+        early_gate(1, "mag3_1")
+        put(2)
+        early_gate(2, "opens2")
+        scale_wear(last)
+        w4_bf = held("w4_bf", [P, N * PACK], BF16)
+        nc.scalar.copy(w4_bf[:].rearrange("p (c i j) -> p c j i", i=4, j=PACK), w4_raw[:].rearrange("p j (c i) -> p c j i", i=4))
+        put(last)
+        opens = opening(last, "opens3")
+
+        w4_w = held("h%d" % last, [P, N], U32)
+        w4_s = held("w4_s", [P, N], U8)
+        nc.vector.quantize_mx(out=w4_w[:].bitcast(FP8X4), scales=w4_s[:], in_=w4_bf[:])
+
+        gate = held("gate0", [P, M], F32)
+        for c in range(HALVES):
+            look(last, opens, gate, BANK * c, BANK)
+        width = BANK // 2
+        q_w = [held("q_w%d" % c, [P, BANK], U32) for c in range(HALVES)]
+        q_s = [held("q_s%d" % c, [P, BANK], U8) for c in range(HALVES)]
+        woven = [held("woven%d" % u, [P, width, 2], F32) for u in range(M // width)]
+        for c in range(HALVES):
+            units = (2 * c, 2 * c + 1)
+            for u in units:
+                cols = slice(width * u, width * (u + 1))
+                nc.vector.scalar_tensor_tensor(
+                    pairs[1][:, cols, 1], gate[:, cols], gain_c[:, last : last + 1], wears[last][:, cols], ALU.mult, ALU.subtract
+                )
+            for u in units:
+                cols = slice(width * u, width * (u + 1))
+                nc.vector.tensor_copy(woven[u][:], both[:, :, cols].rearrange("p u m -> p m u"))
+            for u in units:
+                part = slice(width * (u % 2), width * (u % 2 + 1))
+                nc.vector.quantize_mx(
+                    out=q_w[c][:, part].bitcast(FP8X4), scales=q_s[c][:, part], in_=woven[u][:].rearrange("p m u -> p (m u)").bitcast(BF16)
+                )
+
+        step = 0
+        for c in range(HALVES):
+            for i in range(N // P):
+                rows = slice(P * i, P * (i + 1))
+                y4 = bank(2 * (step % 4))
+                y3 = bank(2 * (step % 4) + 1)
+                for acc, codes, scales in ((y4, w4_w, w4_s), (y3, w3_w, w3_s)):
+                    nc.tensor.matmul_mx(
+                        out=acc[:], lhsT=codes[:, rows].bitcast(FP8X4), lhsT_scale=scales[:, rows],
+                        rhs=q_w[c][:].bitcast(FP8X4), rhs_scale=q_s[c][:], start=True, stop=True,
+                    )
+                y4_sb = held("y4_sb%d" % step, [P, BANK], F32)
+                nc.scalar.copy(y4_sb[:], y4[:])
+                prod = held("prod%d" % step, [P, BANK], F32)
+                nc.vector.tensor_tensor(prod[:], y3[:], y4_sb[:], ALU.mult)
+                if step < 4:
+                    nc.gpsimd.tensor_scalar(y4_sb[:], prod[:], bias_c[:, i : i + 1], 1.0, ALU.add, ALU.mult)
+                else:
+                    nc.scalar.activation(y4_sb[:], prod[:], ACT.Identity, bias=bias_c[:, i : i + 1])
+                nc.sync.dma_start(out[rows, BANK * c : BANK * (c + 1)], y4_sb[:])
+                step = step + 1

@@ -45,15 +45,21 @@ def tile_list_shedding_alarms_kernel(
         def entries(offsets, first, count):
             return offsets[:, first // 16 : (first + count) // 16]
 
-        tab_s = held("tab_s", [P, PASSES * T], U8)
-        nc.vector.memset(tab_s[:].bitcast(I32), 0)
         w2s_raw = held("w2s_raw", [P, PASSES * H], U8)
-        nc.vector.memset(w2s_raw[:].bitcast(I32), 0)
+        nc.gpsimd.memset(w2s_raw[:].bitcast(I32), 0)
+        tab_s = held("tab_s", [P, PASSES * T], U8)
+        nc.vector.memset(tab_s[:, :T].bitcast(I32), 0)
+        nc.gpsimd.memset(tab_s[:, T:].bitcast(I32), 0)
         w3_s = held("w3_s", [P, N], U8)
         nc.vector.memset(w3_s[:].bitcast(I32), 0)
 
         list1 = held("list1", [P, S // 16], U16)
         nc.sync.dma_start(list1[:], offs)
+        for q in range(QUADS):
+            nc.sync.dma_start(
+                w2s_raw[32 * q : 32 * q + 4, :].bitcast(I32).rearrange("r (a c) -> r a c", a=PASSES),
+                w2_scales[:, 4 * q : 4 * q + 4, :].bitcast(I32).rearrange("a r c -> r a c"),
+            )
         tab_w = [held("tab_w%d" % a, [P, T], U32) for a in range(PASSES)]
 
         def load_table(a):
@@ -61,25 +67,20 @@ def tile_list_shedding_alarms_kernel(
 
         load_table(0)
         for q in range(QUADS):
-            nc.gpsimd.dma_start(
+            nc.sync.dma_start(
                 tab_s[32 * q : 32 * q + 4, :].bitcast(I32).rearrange("r (a c) -> r a c", a=PASSES),
                 tab_scales[:, 4 * q : 4 * q + 4, :].bitcast(I32).rearrange("a r c -> r a c"),
             )
-        for q in range(QUADS):
-            nc.scalar.dma_start(
-                w2s_raw[32 * q : 32 * q + 4, :].bitcast(I32).rearrange("r (a c) -> r a c", a=PASSES),
-                w2_scales[:, 4 * q : 4 * q + 4, :].bitcast(I32).rearrange("a r c -> r a c"),
-            )
         ident = held("ident", [P, P], F32)
         make_identity(nc, ident[:])
-        w1_rows = w1.rearrange("(a p j) c -> a p j c", a=PASSES, j=PACK)
-        w1_raw0 = held("w1_raw0", [P, PACK, H], F32)
-        nc.sync.dma_start(w1_raw0[:], w1_rows[0])
         w2w_raw = held("w2w_raw", [P, PASSES * H], U16)
         nc.sync.dma_start(
             w2w_raw[:].bitcast(I32).rearrange("p (a c) -> p a c", a=PASSES),
             w2_words.bitcast(I32).rearrange("a p c -> p a c"),
         )
+        w1_rows = w1.rearrange("(a p j) c -> a p j c", a=PASSES, j=PACK)
+        w1_raw0 = held("w1_raw0", [P, PACK, H], F32)
+        nc.sync.dma_start(w1_raw0[:], w1_rows[0])
         load_table(1)
         w1_raw1 = [held("w1_raw1_%d" % u, [P, PACK, H // 2], F32) for u in range(2)]
         for u in range(2):
@@ -107,6 +108,11 @@ def tile_list_shedding_alarms_kernel(
             for c in range(HALVES):
                 nc.vector.tensor_copy(v_w[a][c][:], tab_w[a][:].indirect(entries(list1, BANK * c, BANK)))
 
+        w2_s = held("w2_s", [P, PASSES * H], U8)
+        nc.vector.tensor_copy(
+            w2_s[:].rearrange("p (a t m) -> p a t m", a=PASSES, t=PACK),
+            w2s_raw[:].rearrange("p (a m t) -> p a t m", a=PASSES, t=PACK),
+        )
         gather_words(0)
         v_planes = [held("v_s%d" % a, [P, S], U8) for a in range(PASSES)]
         for a in range(PASSES):
@@ -138,21 +144,16 @@ def tile_list_shedding_alarms_kernel(
             nc.sync.dma_start(bias_c[:], bias.rearrange("(c p) -> p c", p=P))
         nc.sync.dma_start(pages[3][:], page_rows[3])
 
-        w2_s = held("w2_s", [P, PASSES * H], U8)
-        nc.gpsimd.tensor_copy(
-            w2_s[:].rearrange("p (a t m) -> p a t m", a=PASSES, t=PACK),
-            w2s_raw[:].rearrange("p (a m t) -> p a t m", a=PASSES, t=PACK),
+        w2_w = held("w2_w", [P, PASSES * H], U16)
+        nc.scalar.copy(
+            w2_w[:].rearrange("p (a t m) -> p a m t", a=PASSES, t=PACK),
+            w2w_raw[:].rearrange("p (a m t) -> p a m t", a=PASSES, t=PACK),
         )
         w1_w = [held("w1_w%d" % a, [P, H], U32) for a in range(PASSES)]
         w1_s = [held("w1_s%d" % a, [P, H], U8) for a in range(PASSES)]
         w1_bf = [held("w1_bf%d" % a, [P, H * PACK], BF16) for a in range(PASSES)]
         dealt = [w1_bf[a][:].rearrange("p (t m j) -> p m j t", t=PACK, j=PACK) for a in range(PASSES)]
         nc.scalar.copy(dealt[0], w1_raw0[:].rearrange("p j (m t) -> p m j t", t=PACK))
-        w2_w = held("w2_w", [P, PASSES * H], U16)
-        nc.scalar.copy(
-            w2_w[:].rearrange("p (a t m) -> p a m t", a=PASSES, t=PACK),
-            w2w_raw[:].rearrange("p (a m t) -> p a m t", a=PASSES, t=PACK),
-        )
         nc.vector.quantize_mx(out=w1_w[0][:].bitcast(FP8X4), scales=w1_s[0][:], in_=w1_bf[0][:])
         gather_words(1)
         for u in range(2):
@@ -175,9 +176,9 @@ def tile_list_shedding_alarms_kernel(
                 start=(a == 0), stop=(a == PASSES - 1),
             )
 
-        def scores_turned(t, c, h):
-            x2 = bank(4 + 2 * c)
-            x1 = bank(5 + 2 * c)
+        def scores_turned(t, c, h, mag):
+            x2 = bank(2 * c)
+            x1 = bank(4 + 2 * c)
             for acc, weight in ((x2, w2_slice), (x1, w1_slice)):
                 for b in range(BANK // P):
                     for a in range(PASSES):
@@ -189,11 +190,10 @@ def tile_list_shedding_alarms_kernel(
                             rhs=codes, rhs_scale=scales,
                             start=(a == 0), stop=(a == PASSES - 1),
                         )
-            mag = held("mag%d_%d" % (t, c), [P, BANK], F32)
-            nc.scalar.activation(mag[:], x2[:], ACT.Abs)
+            nc.scalar.activation(mag, x2[:], ACT.Abs)
             neg = ring.tile([P, BANK], F32, name="neg")
             nc.scalar.activation(neg[:], x1[:], ACT.Copy, scale=-1.0)
-            total = bank(c)
+            total = bank(5 + 2 * c)
             for b in range(BANK // P):
                 block = slice(P * b, P * (b + 1))
                 nc.tensor.matmul(total[:, block], mag[:, block], ident[:], start=True, stop=False, is_transpose=True)
@@ -201,27 +201,26 @@ def tile_list_shedding_alarms_kernel(
             nc.scalar.activation(h[:, BANK * c : BANK * (c + 1)], total[:], ACT.Copy, scale=-1.0)
 
         first = [(bank(2 * c), bank(2 * c + 1)) for c in range(HALVES)]
-        mags = []
+        mag_first = held("w1_raw1_1", [P, S], F32)
         for c in range(HALVES):
             x2, x1 = first[c]
             direct_pass(x2, w2_slice, 0, c)
             direct_pass(x1, w1_slice, 0, c)
             direct_pass(x2, w2_slice, 1, c)
-            mag = ring.tile([P, BANK], F32, name="mag")
-            nc.scalar.activation(mag[:], x2[:], ACT.Abs)
-            mags.append(mag)
+            nc.scalar.activation(mag_first[:, BANK * c : BANK * (c + 1)], x2[:], ACT.Abs)
         for c in range(HALVES):
             direct_pass(first[c][1], w1_slice, 1, c)
         for c in range(HALVES):
             h = held("h_first", [P, BANK], F32)
-            nc.vector.tensor_tensor(h[:], first[c][1][:], mags[c][:], ALU.subtract)
+            nc.vector.tensor_tensor(h[:], first[c][1][:], mag_first[:, BANK * c : BANK * (c + 1)], ALU.subtract)
             if c == 0:
                 nc.vector.quantize_mx(out=w1_w[1][:, P:].bitcast(FP8X4), scales=w1_s[1][:, P:], in_=w1_bf[1][:, P * PACK :])
             nc.vector.tensor_tensor(pages[0][:].indirect(entries(list2, BANK * c, BANK)), h[:], wg_first[c][:], ALU.mult)
         last = PACK - 1
         hs = [None] + [held("h%d" % t, [P, S], F32) for t in range(1, PACK)]
         nshare = held("nshare", [P, PACK], F32)
-        nc.gpsimd.tensor_tensor(nshare[:], slope_c[:], share_c[:], ALU.mult)
+        for t in range(PACK):
+            nc.scalar.activation(nshare[:, t : t + 1], slope_c[:, t : t + 1], ACT.Copy, scale=share_c[:, t : t + 1])
         paired = held("paired", [P, PACK // 2, M * 2], BF16)
         pairs = [paired[:, u, :].rearrange("p (m e) -> p m e", e=2) for u in range(PACK // 2)]
         both = paired[:].bitcast(F32)
@@ -250,31 +249,44 @@ def tile_list_shedding_alarms_kernel(
             opens = opening(t, name)
             gate = held("gate%d" % (t % 2), [P, M], F32)
             look(t, opens, gate, 0, M)
-            nc.scalar.activation(gate[:], gate[:], ACT.Copy, scale=gain_c[:, t : t + 1])
-            scale_wear(t)
-            nc.gpsimd.tensor_tensor(pairs[t // 2][:, :, t % 2], gate[:], wears[t][:], ALU.subtract)
+            return gate
 
-        for t in (1, 2):
+        def early_differ(t, gate):
+            flat = held("h%d" % (t + 1), [P, M], BF16)
+            nc.vector.scalar_tensor_tensor(flat[:], gate[:], gain_c[:, t : t + 1], wears[t][:], ALU.mult, ALU.subtract)
+            nc.scalar.copy(pairs[t // 2][:, :, t % 2], flat[:])
+
+        def slice_turned(t, name):
+            mag = held(name, [P, S], F32)
             for c in range(HALVES):
-                scores_turned(t, c, hs[t])
-        early_gate(0, "mag2_1")
-        for c in range(HALVES):
-            scores_turned(last, c, hs[last])
+                scores_turned(t, c, hs[t], mag[:, BANK * c : BANK * (c + 1)])
+
+        slice_turned(1, "w1_bf1")
+        slice_turned(2, "mag2")
+        gate = early_gate(0, "mag2")
+        scale_wear(0)
+        slice_turned(last, "mag3")
         put(1)
-        early_gate(1, "mag3_1")
+        early_differ(0, gate)
+        gate = early_gate(1, "mag3")
+        scale_wear(1)
         put(2)
-        early_gate(2, "opens2")
+        early_differ(1, gate)
+        gate = early_gate(2, "opens2")
         scale_wear(last)
         w4_bf = held("w4_bf", [P, N * PACK], BF16)
         nc.scalar.copy(w4_bf[:].rearrange("p (c i j) -> p c j i", i=4, j=PACK), w4_raw[:].rearrange("p j (c i) -> p c j i", i=4))
         put(last)
+        late_wear = held("h%d" % last, [P, M], F32)
+        nc.scalar.activation(late_wear[:], wears[2][:], ACT.Copy, scale=gain_c[:, 2:3])
         opens = opening(last, "opens3")
+        nc.vector.scalar_tensor_tensor(pairs[1][:, :, 0], gate[:], gain_c[:, 2:3], late_wear[:], ALU.mult, ALU.subtract)
 
-        w4_w = held("h%d" % last, [P, N], U32)
+        w4_w = held("wg_rest", [P, N], U32)
         w4_s = held("w4_s", [P, N], U8)
         nc.vector.quantize_mx(out=w4_w[:].bitcast(FP8X4), scales=w4_s[:], in_=w4_bf[:])
 
-        gate = held("gate0", [P, M], F32)
+        gate = held("gate1", [P, M], F32)
         for c in range(HALVES):
             look(last, opens, gate, BANK * c, BANK)
         width = BANK // 2
@@ -310,7 +322,7 @@ def tile_list_shedding_alarms_kernel(
                     )
                 y4_sb = held("y4_sb%d" % step, [P, BANK], F32)
                 nc.scalar.copy(y4_sb[:], y4[:])
-                prod = held("prod%d" % step, [P, BANK], F32)
+                prod = held("woven3" if step == 0 else "prod%d" % step, [P, BANK], F32)
                 nc.vector.tensor_tensor(prod[:], y3[:], y4_sb[:], ALU.mult)
                 if step < 4:
                     nc.gpsimd.tensor_scalar(y4_sb[:], prod[:], bias_c[:, i : i + 1], 1.0, ALU.add, ALU.mult)

@@ -22,7 +22,7 @@ P = 128
 PACK = 4
 PASSES = K // (P * PACK)
 BANK = 512
-QUADS = 4
+QUAD_ORDER = (0, 2, 1, 3)
 HALVES = S // BANK
 
 
@@ -33,7 +33,6 @@ def tile_list_shedding_alarms_kernel(
     nc = tc.nc
     with ExitStack() as ctx:
         keep = ctx.enter_context(tc.tile_pool(name="keep", bufs=1))
-        ring = ctx.enter_context(tc.tile_pool(name="ring", bufs=2))
         psum = ctx.enter_context(tc.psum_pool(name="psum", bufs=1))
 
         def held(name, shape, dtype):
@@ -55,7 +54,7 @@ def tile_list_shedding_alarms_kernel(
 
         list1 = held("list1", [P, S // 16], U16)
         nc.sync.dma_start(list1[:], offs)
-        for q in range(QUADS):
+        for q in QUAD_ORDER:
             nc.sync.dma_start(
                 w2s_raw[32 * q : 32 * q + 4, :].bitcast(I32).rearrange("r (a c) -> r a c", a=PASSES),
                 w2_scales[:, 4 * q : 4 * q + 4, :].bitcast(I32).rearrange("a r c -> r a c"),
@@ -66,7 +65,7 @@ def tile_list_shedding_alarms_kernel(
             nc.sync.dma_start(tab_w[a][:].bitcast(I32), tab_words[a].rearrange("p t i -> p (t i)").bitcast(I32))
 
         load_table(0)
-        for q in range(QUADS):
+        for q in QUAD_ORDER:
             nc.sync.dma_start(
                 tab_s[32 * q : 32 * q + 4, :].bitcast(I32).rearrange("r (a c) -> r a c", a=PASSES),
                 tab_scales[:, 4 * q : 4 * q + 4, :].bitcast(I32).rearrange("a r c -> r a c"),
@@ -91,7 +90,7 @@ def tile_list_shedding_alarms_kernel(
         wg_first = [held("wg_first%d" % c, [P, BANK], F32) for c in range(HALVES)]
 
         def load_first_weights(c):
-            for q in (0, 2, 1, 3):
+            for q in QUAD_ORDER:
                 nc.sync.dma_start(wg_first[c][32 * q : 32 * q + 32, :], wgs_rows[:, 0, BANK * c : BANK * (c + 1)])
 
         load_first_weights(0)
@@ -118,9 +117,9 @@ def tile_list_shedding_alarms_kernel(
         for a in range(PASSES):
             nc.vector.tensor_copy(v_planes[a][:], tab_s[:, T * a : T * (a + 1)].indirect(list1[:]))
 
-        wg_rest = held("wg_rest", [P, PACK - 1, S], F32)
-        for q in (0, 2, 1, 3):
-            nc.sync.dma_start(wg_rest[32 * q : 32 * q + 32, :, :], wgs_rows[:, 1:, :])
+        wg_second = held("wg_second", [P, S], F32)
+        for q in QUAD_ORDER:
+            nc.sync.dma_start(wg_second[32 * q : 32 * q + 32, :], wgs_rows[:, 1, :])
         nc.sync.dma_start(pages[1][:], page_rows[1])
         list3 = held("list3", [P, M // 16], U16)
         nc.sync.dma_start(list3[:], offs3)
@@ -130,6 +129,9 @@ def tile_list_shedding_alarms_kernel(
         for col, vec in ((slope_c, slope), (share_c, share), (gain_c, gain)):
             nc.sync.dma_start(col[:], vec.rearrange("(p t) -> p t", t=PACK))
         nc.sync.dma_start(wears[0][:], wear_rows[0])
+        wg_rest = held("wg_rest", [P, 2, S], F32)
+        for q in QUAD_ORDER:
+            nc.sync.dma_start(wg_rest[32 * q : 32 * q + 32, :, :], wgs_rows[:, 2:, :])
         nc.sync.dma_start(pages[2][:], page_rows[2])
         for t in range(1, PACK):
             nc.sync.dma_start(wears[t][:], wear_rows[t])
@@ -137,7 +139,7 @@ def tile_list_shedding_alarms_kernel(
         nc.sync.dma_start(w4_raw[:], w4.rearrange("(p j) c -> p j c", j=PACK))
         w3_w = held("w3_w", [P, N], U32)
         nc.sync.dma_start(w3_w[:].bitcast(I32), w3_words[0].rearrange("p c i -> p (c i)").bitcast(I32))
-        for q in range(QUADS):
+        for q in QUAD_ORDER:
             nc.sync.dma_start(w3_s[32 * q : 32 * q + 4, :].bitcast(I32), w3_scales[0, 4 * q : 4 * q + 4, :].bitcast(I32))
         bias_c = held("bias_c", [P, N // P], F32)
         with nc.allow_non_contiguous_dma(reason="one value a partition"):
@@ -176,7 +178,7 @@ def tile_list_shedding_alarms_kernel(
                 start=(a == 0), stop=(a == PASSES - 1),
             )
 
-        def scores_turned(t, c, h, mag):
+        def scores_turned(t, c, h, mag, neg):
             x2 = bank(2 * c)
             x1 = bank(4 + 2 * c)
             for acc, weight in ((x2, w2_slice), (x1, w1_slice)):
@@ -191,8 +193,7 @@ def tile_list_shedding_alarms_kernel(
                             start=(a == 0), stop=(a == PASSES - 1),
                         )
             nc.scalar.activation(mag, x2[:], ACT.Abs)
-            neg = ring.tile([P, BANK], F32, name="neg")
-            nc.scalar.activation(neg[:], x1[:], ACT.Copy, scale=-1.0)
+            nc.scalar.activation(neg, x1[:], ACT.Copy, scale=-1.0)
             total = bank(5 + 2 * c)
             for b in range(BANK // P):
                 block = slice(P * b, P * (b + 1))
@@ -221,9 +222,6 @@ def tile_list_shedding_alarms_kernel(
         nshare = held("nshare", [P, PACK], F32)
         for t in range(PACK):
             nc.scalar.activation(nshare[:, t : t + 1], slope_c[:, t : t + 1], ACT.Copy, scale=share_c[:, t : t + 1])
-        paired = held("paired", [P, PACK // 2, M * 2], BF16)
-        pairs = [paired[:, u, :].rearrange("p (m e) -> p m e", e=2) for u in range(PACK // 2)]
-        both = paired[:].bitcast(F32)
         tops = held("tops", [P, PACK], F32)
 
         def opening(t, name):
@@ -240,7 +238,7 @@ def tile_list_shedding_alarms_kernel(
             )
 
         def put(t):
-            nc.vector.tensor_tensor(pages[t][:].indirect(list2[:]), hs[t][:], wg_rest[:, t - 1, :], ALU.mult)
+            nc.vector.tensor_tensor(pages[t][:].indirect(list2[:]), hs[t][:], wg_second[:] if t == 1 else wg_rest[:, t - 2, :], ALU.mult)
 
         def scale_wear(t):
             nc.scalar.activation(wears[t][:], wears[t][:], ACT.Copy, scale=gain_c[:, t : t + 1])
@@ -252,24 +250,25 @@ def tile_list_shedding_alarms_kernel(
             return gate
 
         def early_differ(t, gate):
-            flat = held("h%d" % (t + 1), [P, M], BF16)
-            nc.vector.scalar_tensor_tensor(flat[:], gate[:], gain_c[:, t : t + 1], wears[t][:], ALU.mult, ALU.subtract)
-            nc.scalar.copy(pairs[t // 2][:, :, t % 2], flat[:])
+            nc.gpsimd.tensor_tensor(wears[t][:], gate[:], wears[t][:], ALU.subtract)
+            nc.scalar.activation(pairs[0][:, :, t], wears[t][:], ACT.Copy, scale=gain_c[:, t : t + 1])
 
         def slice_turned(t, name):
             mag = held(name, [P, S], F32)
+            neg = held("neg%d" % t, [P, S], F32)
             for c in range(HALVES):
-                scores_turned(t, c, hs[t], mag[:, BANK * c : BANK * (c + 1)])
+                scores_turned(t, c, hs[t], mag[:, BANK * c : BANK * (c + 1)], neg[:, BANK * c : BANK * (c + 1)])
 
         slice_turned(1, "w1_bf1")
         slice_turned(2, "mag2")
-        gate = early_gate(0, "mag2")
-        scale_wear(0)
+        gate = early_gate(0, "neg2")
         slice_turned(last, "mag3")
+        paired = held("mag3", [P, PACK // 2, M * 2], BF16)
+        pairs = [paired[:, u, :].rearrange("p (m e) -> p m e", e=2) for u in range(PACK // 2)]
+        both = paired[:].bitcast(F32)
         put(1)
         early_differ(0, gate)
-        gate = early_gate(1, "mag3")
-        scale_wear(1)
+        gate = early_gate(1, "neg3")
         put(2)
         early_differ(1, gate)
         gate = early_gate(2, "opens2")
@@ -323,10 +322,13 @@ def tile_list_shedding_alarms_kernel(
                 y4_sb = held("y4_sb%d" % step, [P, BANK], F32)
                 nc.scalar.copy(y4_sb[:], y4[:])
                 prod = held("woven3" if step == 0 else "prod%d" % step, [P, BANK], F32)
-                nc.vector.tensor_tensor(prod[:], y3[:], y4_sb[:], ALU.mult)
-                if step < 4:
-                    nc.gpsimd.tensor_scalar(y4_sb[:], prod[:], bias_c[:, i : i + 1], 1.0, ALU.add, ALU.mult)
-                else:
-                    nc.scalar.activation(y4_sb[:], prod[:], ACT.Identity, bias=bias_c[:, i : i + 1])
-                nc.sync.dma_start(out[rows, BANK * c : BANK * (c + 1)], y4_sb[:])
+                pieces = 2 if step == 5 else 1
+                for piece in range(pieces):
+                    cols = slice(BANK // pieces * piece, BANK // pieces * (piece + 1))
+                    nc.vector.tensor_tensor(prod[:, cols], y3[:, cols], y4_sb[:, cols], ALU.mult)
+                    if step < 4:
+                        nc.gpsimd.tensor_scalar(y4_sb[:, cols], prod[:, cols], bias_c[:, i : i + 1], 1.0, ALU.add, ALU.mult)
+                    else:
+                        nc.scalar.activation(y4_sb[:, cols], prod[:, cols], ACT.Identity, bias=bias_c[:, i : i + 1])
+                    nc.sync.dma_start(out[rows, BANK * c + cols.start : BANK * c + cols.stop], y4_sb[:, cols])
                 step = step + 1

@@ -137,6 +137,7 @@ def tile_list_shedding_alarms_kernel(
             nc.sync.dma_start(wears[t][:], wear_rows[t])
         w4_raw = held("w4_raw", [P, PACK, N], F32)
         nc.sync.dma_start(w4_raw[:], w4.rearrange("(p j) c -> p j c", j=PACK))
+        nc.sync.dma_start(pages[3][:], page_rows[3])
         w3_w = held("w3_w", [P, N], U32)
         nc.sync.dma_start(w3_w[:].bitcast(I32), w3_words[0].rearrange("p c i -> p (c i)").bitcast(I32))
         for q in QUAD_ORDER:
@@ -144,7 +145,6 @@ def tile_list_shedding_alarms_kernel(
         bias_c = held("bias_c", [P, N // P], F32)
         with nc.allow_non_contiguous_dma(reason="one value a partition"):
             nc.sync.dma_start(bias_c[:], bias.rearrange("(c p) -> p c", p=P))
-        nc.sync.dma_start(pages[3][:], page_rows[3])
 
         w2_w = held("w2_w", [P, PASSES * H], U16)
         nc.scalar.copy(
@@ -170,8 +170,8 @@ def tile_list_shedding_alarms_kernel(
             rows = slice(H * a + P * t, H * a + P * (t + 1))
             return w2_w[:, rows].bitcast(FP4X4), w2_s[:, rows]
 
-        def direct_pass(acc, weight, a, c):
-            codes, scales = weight(a, 0)
+        def direct_pass(acc, weight, a, c, t=0):
+            codes, scales = weight(a, t)
             nc.tensor.matmul_mx(
                 out=acc[:], lhsT=codes, lhsT_scale=scales,
                 rhs=v_w[a][c][:].bitcast(FP8X4), rhs_scale=v_planes[a][:, BANK * c : BANK * (c + 1)],
@@ -179,8 +179,8 @@ def tile_list_shedding_alarms_kernel(
             )
 
         def scores_turned(t, c, h, mag, neg):
-            x2 = bank(2 * c)
-            x1 = bank(4 + 2 * c)
+            x2 = bank(4)
+            x1 = bank(1 + 2 * c)
             for acc, weight in ((x2, w2_slice), (x1, w1_slice)):
                 for b in range(BANK // P):
                     for a in range(PASSES):
@@ -194,14 +194,14 @@ def tile_list_shedding_alarms_kernel(
                         )
             nc.scalar.activation(mag, x2[:], ACT.Abs)
             nc.scalar.activation(neg, x1[:], ACT.Copy, scale=-1.0)
-            total = bank(5 + 2 * c)
+            total = bank(6 + c)
             for b in range(BANK // P):
                 block = slice(P * b, P * (b + 1))
                 nc.tensor.matmul(total[:, block], mag[:, block], ident[:], start=True, stop=False, is_transpose=True)
                 nc.tensor.matmul(total[:, block], neg[:, block], ident[:], start=False, stop=True, is_transpose=True)
             nc.scalar.activation(h[:, BANK * c : BANK * (c + 1)], total[:], ACT.Copy, scale=-1.0)
 
-        first = [(bank(2 * c), bank(2 * c + 1)) for c in range(HALVES)]
+        first = [(bank(4 - 2 * c), bank(2 * c + 1)) for c in range(HALVES)]
         mag_first = held("w1_raw1_1", [P, S], F32)
         for c in range(HALVES):
             x2, x1 = first[c]
@@ -218,7 +218,7 @@ def tile_list_shedding_alarms_kernel(
                 nc.vector.quantize_mx(out=w1_w[1][:, P:].bitcast(FP8X4), scales=w1_s[1][:, P:], in_=w1_bf[1][:, P * PACK :])
             nc.vector.tensor_tensor(pages[0][:].indirect(entries(list2, BANK * c, BANK)), h[:], wg_first[c][:], ALU.mult)
         last = PACK - 1
-        hs = [None] + [held("h%d" % t, [P, S], F32) for t in range(1, PACK)]
+        hs = [None, held("wg_first1", [P, S], F32)] + [held("h%d" % t, [P, S], F32) for t in range(2, PACK)]
         nshare = held("nshare", [P, PACK], F32)
         for t in range(PACK):
             nc.scalar.activation(nshare[:, t : t + 1], slope_c[:, t : t + 1], ACT.Copy, scale=share_c[:, t : t + 1])
@@ -259,8 +259,16 @@ def tile_list_shedding_alarms_kernel(
             for c in range(HALVES):
                 scores_turned(t, c, hs[t], mag[:, BANK * c : BANK * (c + 1)], neg[:, BANK * c : BANK * (c + 1)])
 
-        slice_turned(1, "w1_bf1")
-        slice_turned(2, "mag2")
+        mag_second = held("mag1", [P, S], F32)
+        for c in range(HALVES):
+            cols = slice(BANK * c, BANK * (c + 1))
+            x2, x1 = bank(2), bank(5 * c)
+            for acc, weight in ((x2, w2_slice), (x1, w1_slice)):
+                for a in range(PASSES):
+                    direct_pass(acc, weight, a, c, 1)
+            nc.scalar.activation(mag_second[:, cols], x2[:], ACT.Abs)
+            nc.vector.tensor_tensor(hs[1][:, cols], x1[:], mag_second[:, cols], ALU.subtract)
+        slice_turned(2, "w1_bf1")
         gate = early_gate(0, "neg2")
         slice_turned(last, "mag3")
         paired = held("mag3", [P, PACK // 2, M * 2], BF16)

from contextlib import ExitStack

import concourse.mybir as mybir
from concourse.masks import make_identity

K, H, N, T, S, T2, M = 1024, 512, 384, 2048, 1024, 2048, 1024
FLOPS = 2 * (2 * K * H * S + 2 * H * N * M)

F32 = mybir.dt.float32
BF16 = mybir.dt.bfloat16
I32 = mybir.dt.int32
U32 = mybir.dt.uint32
U16 = mybir.dt.uint16
U8 = mybir.dt.uint8
FP8X4 = mybir.dt.float8_e4m3fn_x4
FP4X4 = mybir.dt.float4_e2m1fn_x4
ACT = mybir.ActivationFunctionType
ALU = mybir.AluOpType
AX = mybir.AxisListType

P = 128
PACK = 4
PASSES = K // (P * PACK)
BANK = 512
QUAD_ORDER = (0, 2, 1, 3)
HALVES = S // BANK


def tile_list_shedding_alarms_kernel(
    tc, tab_words, tab_scales, offs, offs2, offs3, w1, w2_words, w2_scales, page0, wgs,
    slope, share, wear, gain, w3_words, w3_scales, w4, bias, out,
):
    nc = tc.nc
    with ExitStack() as ctx:
        keep = ctx.enter_context(tc.tile_pool(name="keep", bufs=1))
        psum = ctx.enter_context(tc.psum_pool(name="psum", bufs=1))

        def held(name, shape, dtype):
            return keep.tile(shape, dtype, name=name, align_bytes=64)

        def bank(number):
            return psum.tile([P, BANK], F32, name="bank%d" % number)

        def entries(offsets, first, count):
            return offsets[:, first // 16 : (first + count) // 16]

        w2s_raw = held("w2s_raw", [P, PASSES * H], U8)
        nc.gpsimd.memset(w2s_raw[:].bitcast(I32), 0)
        tab_s = held("tab_s", [P, PASSES * T], U8)
        nc.vector.memset(tab_s[:, :T].bitcast(I32), 0)
        nc.gpsimd.memset(tab_s[:, T:].bitcast(I32), 0)
        w3_s = held("w3_s", [P, N], U8)
        nc.vector.memset(w3_s[:].bitcast(I32), 0)

        list1 = held("list1", [P, S // 16], U16)
        nc.sync.dma_start(list1[:], offs)
        for q in QUAD_ORDER:
            nc.sync.dma_start(
                w2s_raw[32 * q : 32 * q + 4, :].bitcast(I32).rearrange("r (a c) -> r a c", a=PASSES),
                w2_scales[:, 4 * q : 4 * q + 4, :].bitcast(I32).rearrange("a r c -> r a c"),
            )
        tab_w = [held("tab_w%d" % a, [P, T], U32) for a in range(PASSES)]

        def load_table(a):
            nc.sync.dma_start(tab_w[a][:].bitcast(I32), tab_words[a].rearrange("p t i -> p (t i)").bitcast(I32))

        load_table(0)
        for q in QUAD_ORDER:
            nc.sync.dma_start(
                tab_s[32 * q : 32 * q + 4, :].bitcast(I32).rearrange("r (a c) -> r a c", a=PASSES),
                tab_scales[:, 4 * q : 4 * q + 4, :].bitcast(I32).rearrange("a r c -> r a c"),
            )
        ident = held("ident", [P, P], F32)
        make_identity(nc, ident[:])
        w2w_raw = held("w2w_raw", [P, PASSES * H], U16)
        nc.sync.dma_start(
            w2w_raw[:].bitcast(I32).rearrange("p (a c) -> p a c", a=PASSES),
            w2_words.bitcast(I32).rearrange("a p c -> p a c"),
        )
        w1_rows = w1.rearrange("(a p j) c -> a p j c", a=PASSES, j=PACK)
        w1_raw0 = held("w1_raw0", [P, PACK, H], F32)
        nc.sync.dma_start(w1_raw0[:], w1_rows[0])
        load_table(1)
        w1_raw1 = [held("w1_raw1_%d" % u, [P, PACK, H // 2], F32) for u in range(2)]
        for u in range(2):
            nc.sync.dma_start(w1_raw1[u][:], w1_rows[1][:, :, H // 2 * u : H // 2 * (u + 1)])
        list2 = held("list2", [P, S // 16], U16)
        nc.sync.dma_start(list2[:], offs2)
        wgs_rows = wgs.rearrange("(i t) c -> i t c", t=PACK)
        wg_first = [held("wg_first%d" % c, [P, BANK], F32) for c in range(HALVES)]

        def load_first_weights(c):
            for q in QUAD_ORDER:
                nc.sync.dma_start(wg_first[c][32 * q : 32 * q + 32, :], wgs_rows[:, 0, BANK * c : BANK * (c + 1)])

        load_first_weights(0)
        page_rows = page0.rearrange("(p t) c -> t p c", t=PACK)
        wear_rows = wear.rearrange("(p t) c -> t p c", t=PACK)
        pages = [held("page%d" % t, [P, T2], F32) for t in range(PACK)]
        wears = [held("wear%d" % t, [P, M], F32) for t in range(PACK)]
        nc.sync.dma_start(pages[0][:], page_rows[0])
        load_first_weights(1)

        v_w = [[held("v_w%d_%d" % (a, c), [P, BANK], U32) for c in range(HALVES)] for a in range(PASSES)]

        def gather_words(a):
            for c in range(HALVES):
                nc.vector.tensor_copy(v_w[a][c][:], tab_w[a][:].indirect(entries(list1, BANK * c, BANK)))

        w2_s = held("w2_s", [P, PASSES * H], U8)
        nc.vector.tensor_copy(
            w2_s[:].rearrange("p (a t m) -> p a t m", a=PASSES, t=PACK),
            w2s_raw[:].rearrange("p (a m t) -> p a t m", a=PASSES, t=PACK),
        )
        gather_words(0)
        v_planes = [held("v_s%d" % a, [P, S], U8) for a in range(PASSES)]
        for a in range(PASSES):
            nc.vector.tensor_copy(v_planes[a][:], tab_s[:, T * a : T * (a + 1)].indirect(list1[:]))

        wg_second = held("wg_second", [P, S], F32)
        for q in QUAD_ORDER:
            nc.sync.dma_start(wg_second[32 * q : 32 * q + 32, :], wgs_rows[:, 1, :])
        nc.sync.dma_start(pages[1][:], page_rows[1])
        list3 = held("list3", [P, M // 16], U16)
        nc.sync.dma_start(list3[:], offs3)
        slope_c = held("slope_c", [P, PACK], F32)
        share_c = held("share_c", [P, PACK], F32)
        gain_c = held("gain_c", [P, PACK], F32)
        for col, vec in ((slope_c, slope), (share_c, share), (gain_c, gain)):
            nc.sync.dma_start(col[:], vec.rearrange("(p t) -> p t", t=PACK))
        nc.sync.dma_start(wears[0][:], wear_rows[0])
        wg_rest = held("wg_rest", [P, 2, S], F32)
        for q in QUAD_ORDER:
            nc.sync.dma_start(wg_rest[32 * q : 32 * q + 32, :, :], wgs_rows[:, 2:, :])
        nc.sync.dma_start(pages[2][:], page_rows[2])
        for t in range(1, PACK):
            nc.sync.dma_start(wears[t][:], wear_rows[t])
        w4_raw = held("w4_raw", [P, PACK, N], F32)
        nc.sync.dma_start(w4_raw[:], w4.rearrange("(p j) c -> p j c", j=PACK))
        nc.sync.dma_start(pages[3][:], page_rows[3])
        w3_w = held("w3_w", [P, N], U32)
        nc.sync.dma_start(w3_w[:].bitcast(I32), w3_words[0].rearrange("p c i -> p (c i)").bitcast(I32))
        for q in QUAD_ORDER:
            nc.sync.dma_start(w3_s[32 * q : 32 * q + 4, :].bitcast(I32), w3_scales[0, 4 * q : 4 * q + 4, :].bitcast(I32))
        bias_c = held("bias_c", [P, N // P], F32)
        with nc.allow_non_contiguous_dma(reason="one value a partition"):
            nc.sync.dma_start(bias_c[:], bias.rearrange("(c p) -> p c", p=P))

        w2_w = held("w2_w", [P, PASSES * H], U16)
        nc.scalar.copy(
            w2_w[:].rearrange("p (a t m) -> p a m t", a=PASSES, t=PACK),
            w2w_raw[:].rearrange("p (a m t) -> p a m t", a=PASSES, t=PACK),
        )
        w1_w = [held("w1_w%d" % a, [P, H], U32) for a in range(PASSES)]
        w1_s = [held("w1_s%d" % a, [P, H], U8) for a in range(PASSES)]
        w1_bf = [held("w1_bf%d" % a, [P, H * PACK], BF16) for a in range(PASSES)]
        dealt = [w1_bf[a][:].rearrange("p (t m j) -> p m j t", t=PACK, j=PACK) for a in range(PASSES)]
        nc.scalar.copy(dealt[0], w1_raw0[:].rearrange("p j (m t) -> p m j t", t=PACK))
        nc.vector.quantize_mx(out=w1_w[0][:].bitcast(FP8X4), scales=w1_s[0][:], in_=w1_bf[0][:])
        gather_words(1)
        for u in range(2):
            nc.scalar.copy(dealt[1][:, P // 2 * u : P // 2 * (u + 1)], w1_raw1[u][:].rearrange("p j (m t) -> p m j t", t=PACK))
        nc.vector.quantize_mx(out=w1_w[1][:, :P].bitcast(FP8X4), scales=w1_s[1][:, :P], in_=w1_bf[1][:, : P * PACK])

        def w1_slice(a, t):
            rows = slice(P * t, P * (t + 1))
            return w1_w[a][:, rows].bitcast(FP8X4), w1_s[a][:, rows]

        def w2_slice(a, t):
            rows = slice(H * a + P * t, H * a + P * (t + 1))
            return w2_w[:, rows].bitcast(FP4X4), w2_s[:, rows]

        def direct_pass(acc, weight, a, c, t=0):
            codes, scales = weight(a, t)
            nc.tensor.matmul_mx(
                out=acc[:], lhsT=codes, lhsT_scale=scales,
                rhs=v_w[a][c][:].bitcast(FP8X4), rhs_scale=v_planes[a][:, BANK * c : BANK * (c + 1)],
                start=(a == 0), stop=(a == PASSES - 1),
            )

        def scores_turned(t, c, h, mag, neg):
            x2 = bank(4)
            x1 = bank(1 + 2 * c)
            for acc, weight in ((x2, w2_slice), (x1, w1_slice)):
                for b in range(BANK // P):
                    for a in range(PASSES):
                        codes, scales = weight(a, t)
                        nc.tensor.matmul_mx(
                            out=acc[:, P * b : P * (b + 1)],
                            lhsT=v_w[a][c][:, P * b : P * (b + 1)].bitcast(FP8X4),
                            lhsT_scale=v_planes[a][:, BANK * c + P * b : BANK * c + P * (b + 1)],
                            rhs=codes, rhs_scale=scales,
                            start=(a == 0), stop=(a == PASSES - 1),
                        )
            nc.scalar.activation(mag, x2[:], ACT.Abs)
            nc.scalar.activation(neg, x1[:], ACT.Copy, scale=-1.0)
            total = bank(6 + c)
            for b in range(BANK // P):
                block = slice(P * b, P * (b + 1))
                nc.tensor.matmul(total[:, block], mag[:, block], ident[:], start=True, stop=False, is_transpose=True)
                nc.tensor.matmul(total[:, block], neg[:, block], ident[:], start=False, stop=True, is_transpose=True)
            nc.scalar.activation(h[:, BANK * c : BANK * (c + 1)], total[:], ACT.Copy, scale=-1.0)

        first = [(bank(4 - 2 * c), bank(2 * c + 1)) for c in range(HALVES)]
        mag_first = held("w1_raw1_1", [P, S], F32)
        for c in range(HALVES):
            x2, x1 = first[c]
            direct_pass(x2, w2_slice, 0, c)
            direct_pass(x1, w1_slice, 0, c)
            direct_pass(x2, w2_slice, 1, c)
            nc.scalar.activation(mag_first[:, BANK * c : BANK * (c + 1)], x2[:], ACT.Abs)
        for c in range(HALVES):
            direct_pass(first[c][1], w1_slice, 1, c)
        for c in range(HALVES):
            h = held("h_first", [P, BANK], F32)
            nc.vector.tensor_tensor(h[:], first[c][1][:], mag_first[:, BANK * c : BANK * (c + 1)], ALU.subtract)
            if c == 0:
                nc.vector.quantize_mx(out=w1_w[1][:, P:].bitcast(FP8X4), scales=w1_s[1][:, P:], in_=w1_bf[1][:, P * PACK :])
            nc.vector.tensor_tensor(pages[0][:].indirect(entries(list2, BANK * c, BANK)), h[:], wg_first[c][:], ALU.mult)
        last = PACK - 1
        hs = [None, held("wg_first1", [P, S], F32)] + [held("h%d" % t, [P, S], F32) for t in range(2, PACK)]
        nshare = held("nshare", [P, PACK], F32)
        for t in range(PACK):
            nc.scalar.activation(nshare[:, t : t + 1], slope_c[:, t : t + 1], ACT.Copy, scale=share_c[:, t : t + 1])
        tops = held("tops", [P, PACK], F32)

        def opening(t, name):
            opens = held(name, [P, 1], F32)
            nc.vector.reduce_max(tops[:, t : t + 1], pages[t][:], AX.X, negate=True)
            nc.scalar.activation(opens[:], tops[:, t : t + 1], ACT.Copy, scale=nshare[:, t : t + 1])
            return opens

        def look(t, opens, gate, first, count):
            nc.scalar.activation(
                gate[:, first : first + count],
                pages[t][:].indirect(entries(list3, first, count)),
                ACT.Sigmoid, bias=opens[:], scale=slope_c[:, t : t + 1],
            )

        def put(t):
            nc.vector.tensor_tensor(pages[t][:].indirect(list2[:]), hs[t][:], wg_second[:] if t == 1 else wg_rest[:, t - 2, :], ALU.mult)

        def scale_wear(t):
            nc.scalar.activation(wears[t][:], wears[t][:], ACT.Copy, scale=gain_c[:, t : t + 1])

        def early_gate(t, name):
            opens = opening(t, name)
            gate = held("gate%d" % (t % 2), [P, M], F32)
            look(t, opens, gate, 0, M)
            return gate

        def early_differ(t, gate):
            nc.gpsimd.tensor_tensor(wears[t][:], gate[:], wears[t][:], ALU.subtract)
            nc.scalar.activation(pairs[0][:, :, t], wears[t][:], ACT.Copy, scale=gain_c[:, t : t + 1])

        def slice_turned(t, name):
            mag = held(name, [P, S], F32)
            neg = held("neg%d" % t, [P, S], F32)
            for c in range(HALVES):
                scores_turned(t, c, hs[t], mag[:, BANK * c : BANK * (c + 1)], neg[:, BANK * c : BANK * (c + 1)])

        mag_second = held("mag1", [P, S], F32)
        for c in range(HALVES):
            cols = slice(BANK * c, BANK * (c + 1))
            x2, x1 = bank(2), bank(5 * c)
            for acc, weight in ((x2, w2_slice), (x1, w1_slice)):
                for a in range(PASSES):
                    direct_pass(acc, weight, a, c, 1)
            nc.scalar.activation(mag_second[:, cols], x2[:], ACT.Abs)
            nc.vector.tensor_tensor(hs[1][:, cols], x1[:], mag_second[:, cols], ALU.subtract)
        slice_turned(2, "w1_bf1")
        gate = early_gate(0, "neg2")
        slice_turned(last, "mag3")
        paired = held("mag3", [P, PACK // 2, M * 2], BF16)
        pairs = [paired[:, u, :].rearrange("p (m e) -> p m e", e=2) for u in range(PACK // 2)]
        both = paired[:].bitcast(F32)
        put(1)
        early_differ(0, gate)
        gate = early_gate(1, "neg3")
        put(2)
        early_differ(1, gate)
        gate = early_gate(2, "opens2")
        scale_wear(last)
        w4_bf = held("w4_bf", [P, N * PACK], BF16)
        nc.scalar.copy(w4_bf[:].rearrange("p (c i j) -> p c j i", i=4, j=PACK), w4_raw[:].rearrange("p j (c i) -> p c j i", i=4))
        put(last)
        late_wear = held("h%d" % last, [P, M], F32)
        nc.scalar.activation(late_wear[:], wears[2][:], ACT.Copy, scale=gain_c[:, 2:3])
        opens = opening(last, "opens3")
        nc.vector.scalar_tensor_tensor(pairs[1][:, :, 0], gate[:], gain_c[:, 2:3], late_wear[:], ALU.mult, ALU.subtract)

        w4_w = held("wg_rest", [P, N], U32)
        w4_s = held("w4_s", [P, N], U8)
        nc.vector.quantize_mx(out=w4_w[:].bitcast(FP8X4), scales=w4_s[:], in_=w4_bf[:])

        gate = held("gate1", [P, M], F32)
        for c in range(HALVES):
            look(last, opens, gate, BANK * c, BANK)
        width = BANK // 2
        q_w = [held("q_w%d" % c, [P, BANK], U32) for c in range(HALVES)]
        q_s = [held("q_s%d" % c, [P, BANK], U8) for c in range(HALVES)]
        woven = [held("woven%d" % u, [P, width, 2], F32) for u in range(M // width)]
        for c in range(HALVES):
            units = (2 * c, 2 * c + 1)
            for u in units:
                cols = slice(width * u, width * (u + 1))
                nc.vector.scalar_tensor_tensor(
                    pairs[1][:, cols, 1], gate[:, cols], gain_c[:, last : last + 1], wears[last][:, cols], ALU.mult, ALU.subtract
                )
            for u in units:
                cols = slice(width * u, width * (u + 1))
                nc.vector.tensor_copy(woven[u][:], both[:, :, cols].rearrange("p u m -> p m u"))
            for u in units:
                part = slice(width * (u % 2), width * (u % 2 + 1))
                nc.vector.quantize_mx(
                    out=q_w[c][:, part].bitcast(FP8X4), scales=q_s[c][:, part], in_=woven[u][:].rearrange("p m u -> p (m u)").bitcast(BF16)
                )

        step = 0
        for c in range(HALVES):
            for i in range(N // P):
                rows = slice(P * i, P * (i + 1))
                y4 = bank(2 * (step % 4))
                y3 = bank(2 * (step % 4) + 1)
                for acc, codes, scales in ((y4, w4_w, w4_s), (y3, w3_w, w3_s)):
                    nc.tensor.matmul_mx(
                        out=acc[:], lhsT=codes[:, rows].bitcast(FP8X4), lhsT_scale=scales[:, rows],
                        rhs=q_w[c][:].bitcast(FP8X4), rhs_scale=q_s[c][:], start=True, stop=True,
                    )
                y4_sb = held("y4_sb%d" % step, [P, BANK], F32)
                nc.scalar.copy(y4_sb[:], y4[:])
                prod = held("woven3" if step == 0 else "prod%d" % step, [P, BANK], F32)
                pieces = 2 if step == 5 else 1
                for piece in range(pieces):
                    cols = slice(BANK // pieces * piece, BANK // pieces * (piece + 1))
                    nc.vector.tensor_tensor(prod[:, cols], y3[:, cols], y4_sb[:, cols], ALU.mult)
                    if step < 4:
                        nc.gpsimd.tensor_scalar(y4_sb[:, cols], prod[:, cols], bias_c[:, i : i + 1], 1.0, ALU.add, ALU.mult)
                    else:
                        nc.scalar.activation(y4_sb[:, cols], prod[:, cols], ACT.Identity, bias=bias_c[:, i : i + 1])
                    nc.sync.dma_start(out[rows, BANK * c + cols.start : BANK * c + cols.stop], y4_sb[:, cols])
                step = step + 1
